import numpy as np
import ml_dtypes


def mxq(x, axis, fmt="e4m3"):
    dtype, down = {"e4m3": (ml_dtypes.float8_e4m3fn, 7), "e5m2": (ml_dtypes.float8_e5m2, 14)}[fmt]
    v = np.moveaxis(np.asarray(x, np.float32).astype(ml_dtypes.bfloat16).astype(np.float64), axis, -1)
    blocks = v.reshape(v.shape[:-1] + (-1, 32))
    amax = np.abs(blocks).max(-1, keepdims=True)
    byte = np.maximum(np.where(amax > 0, np.frexp(amax)[1] - 1 + 127, 0) - down, 1)
    scale = np.exp2(byte - 127.0)
    codes = (blocks / scale).astype(np.float32).astype(dtype).astype(np.float64)
    return np.moveaxis((codes * scale).reshape(v.shape), -1, axis)


WIDE = False


def mx_kscale(k):
    if not WIDE:
        return np.ones(k)
    levels = np.array([30, -30])
    if k % 512:
        return np.exp2(np.random.permutation(np.resize(levels, k // 32))).repeat(32)
    a = np.empty((k // 512, 16))
    for p in range(k // 512):
        a[p, :8] = np.random.permutation(np.resize(levels, 8))
        for g in range(8):
            far = levels[np.abs(levels - a[p, g]) >= 10]
            a[p, g + 8] = far[np.random.randint(len(far))]
    return np.exp2(a.ravel()).repeat(32)


def f64(x):
    return np.asarray(x).astype(np.float64)


def striped(idx):
    return np.tile(np.asarray(idx).reshape(-1, 16).T, (8, 1)).astype(np.uint16)


def unstriped(offs):
    return offs[:16].T.reshape(-1).astype(np.int64)


E2M1 = np.array([0.0, 0.5, 1.0, 1.5, 2.0, 3.0, 4.0, 6.0, -0.0, -0.5, -1.0, -1.5, -2.0, -3.0, -4.0, -6.0])


def pack_weight(w, fmt):
    k, n = w.shape
    w = f64(np.asarray(w, np.float32).astype(ml_dtypes.bfloat16)).reshape(k // 32, 32, n)
    amax = np.abs(w).max(1)
    if fmt in ("e4m3", "e5m2"):
        byte = np.frexp(amax)[1] - 1 + 127 - (7 if fmt == "e4m3" else 14)
    else:
        mant, ex = np.frexp(amax / 6.0)
        byte = np.where(mant > 0.5, ex, ex - 1) + 127
    byte = np.clip(np.where(amax > 0, byte, 1), 1, 254)
    scaled = (w * np.exp2(127.0 - byte)[:, None, :]).reshape(k, n).astype(np.float32)
    by_word = np.ascontiguousarray(scaled.reshape(k // 512, 128, 4, n).transpose(0, 1, 3, 2))
    if fmt in ("e4m3", "e5m2"):
        words = by_word.astype(ml_dtypes.float8_e4m3fn if fmt == "e4m3" else ml_dtypes.float8_e5m2).view(np.uint8)
    else:
        c = by_word.astype(ml_dtypes.float4_e2m1fn).view(np.uint8) & 0xF
        words = (c[..., 0::2] | (c[..., 1::2] << 4)).reshape(k // 512, 128, 2 * n)
    return np.ascontiguousarray(words), np.ascontiguousarray(byte.astype(np.uint8).reshape(k // 512, 16, n))


def unpack_weight(words, scales, fmt):
    g, _, n = scales.shape
    words = np.ascontiguousarray(words).reshape(g, 128, n, -1)
    if fmt in ("e4m3", "e5m2"):
        vals = words.view(ml_dtypes.float8_e4m3fn if fmt == "e4m3" else ml_dtypes.float8_e5m2).astype(np.float64)
    else:
        nib = np.empty((g, 128, n, 4), np.uint8)
        nib[..., 0::2] = words & 0xF
        nib[..., 1::2] = words >> 4
        vals = E2M1[nib]
    vals = vals * np.repeat(np.exp2(scales.astype(np.float64) - 127.0), 8, axis=1)[..., None]
    return vals.transpose(0, 1, 3, 2).reshape(g * 512, n)


def sigmoid(v):
    return 1.0 / (1.0 + np.exp(-v))


def sgn(shape):
    return np.random.uniform(0.5, 2.0, shape) * np.where(np.random.standard_normal(shape) < 0, -1.0, 1.0)


K, T, J, R, V, C, O, N, U = 512, 1024, 256, 512, 1024, 512, 256, 256, 128


def setup_inputs():
    n = np.random.standard_normal
    idx = np.random.permutation(V)[:R]
    idx2 = np.random.permutation(T)[:J]
    idx3 = np.random.permutation(C)[:J]
    idx4 = np.random.permutation(C)[:O]
    idx5 = np.random.permutation(C)[:O]
    idx6 = np.random.permutation(O)[:U]
    idx7 = np.random.permutation(O)[:U]
    fk = mx_kscale(K)
    fr = mx_kscale(R)
    xtp = pack_weight(n((K, T)) / fk[:, None], "e2m1")
    wtp = pack_weight(n((K, V)) * 1 / np.sqrt(K) * fk[:, None], "e5m2")
    wbp = pack_weight(n((R, N)) * 1 / np.sqrt(R) / fr[:, None], "e4m3")
    return {
        "xt_words": xtp[0],
        "xt_scales": xtp[1],
        "wt_words": wtp[0],
        "wt_scales": wtp[1],
        "sa": (np.random.uniform(0.5, 1.6, (R, 1)) * fr[:, None]).astype(np.float32),
        "sg": (sgn((R, 1))).astype(np.float32),
        "bg": (np.random.uniform(-2.0, 2.0, (R, 1))).astype(np.float32),
        "wb_words": wbp[0],
        "wb_scales": wbp[1],
        "so": (np.random.uniform(0.5, 1.6, (N, 1))).astype(np.float32),
        "offs": striped(idx),
        "offs2": striped(idx2),
        "offs3": striped(idx3),
        "offs4": striped(idx4),
        "offs5": striped(idx5),
        "offs6": striped(idx6),
        "offs7": striped(idx7),
    }


def reference(xt_words, xt_scales, wt_words, wt_scales, sa, sg, bg, wb_words, wb_scales, so, offs, offs2, offs3, offs4, offs5, offs6, offs7):
    idx = unstriped(offs)
    idx2 = unstriped(offs2)
    idx3 = unstriped(offs3)
    idx4 = unstriped(offs4)
    idx5 = unstriped(offs5)
    idx6 = unstriped(offs6)
    idx7 = unstriped(offs7)
    xtu = unpack_weight(xt_words, xt_scales, "e2m1")
    wtu = unpack_weight(wt_words, wt_scales, "e5m2")
    wbu = unpack_weight(wb_words, wb_scales, "e4m3")
    wtidxg = wtu[:, idx]
    xtidx2g = xtu[:, idx2]
    a = wtidxg.T @ xtidx2g
    pw = np.zeros((R, C))
    pw[:, idx3] = a
    hid = pw[:, idx4] * f64(sa) * sigmoid(pw[:, idx5] * f64(sg) + f64(bg))
    hidq = mxq(hid, 0, "e5m2")
    p = wbu.T @ hidq
    y = p[:, idx6] - p[:, idx7] * f64(so)
    return y

@@ -1,0 +1,177 @@
+from contextlib import ExitStack
+
+import concourse.mybir as mybir
+
+K, T, J, R, V, C, O, N, U = 512, 1024, 256, 512, 1024, 512, 256, 256, 128
+FLOPS = 2 * K * R * J + 2 * R * N * O
+
+F32 = mybir.dt.float32
+BF16 = mybir.dt.bfloat16
+I32 = mybir.dt.int32
+U32 = mybir.dt.uint32
+U16 = mybir.dt.uint16
+U8 = mybir.dt.uint8
+E2M1 = mybir.dt.float4_e2m1fn_x4
+E4M3 = mybir.dt.float8_e4m3fn_x4
+E5M2 = mybir.dt.float8_e5m2_x4
+ACT = mybir.ActivationFunctionType
+ALU = mybir.AluOpType
+
+P = 128
+PACK = 4
+QUADS = 4
+HALF = O // 2
+
+
+def tile_list_gatedread_chosen_one_weighedout_kernel(
+    tc, xt_words, xt_scales, wt_words, wt_scales, sa, sg, bg, wb_words, wb_scales, so,
+    offs, offs2, offs3, offs4, offs5, offs6, offs7, out,
+):
+    nc = tc.nc
+    with ExitStack() as ctx:
+        pool = ctx.enter_context(tc.tile_pool(name="pool", bufs=1))
+        psum = ctx.enter_context(tc.psum_pool(name="psum", bufs=1))
+
+        def load_list(name, src):
+            lst = pool.tile(list(src.shape), U16, name=name)
+            nc.sync.dma_start(lst[:], src)
+            return lst
+
+        def zeroed_scales(engine, name, width):
+            rows = pool.tile([P, width], U8, name=name, align_bytes=64)
+            engine.memset(rows[:].bitcast(I32), 0)
+            return rows
+
+        def load_scales(queue, rows, src):
+            for q in range(QUADS):
+                queue.dma_start(rows[32 * q : 32 * q + 4, :].bitcast(I32), src[0, 4 * q : 4 * q + 4, :].bitcast(I32))
+
+        def load_rowwise(name, src):
+            col = pool.tile([P, PACK], F32, name=name)
+            nc.gpsimd.dma_start(col[:], src.rearrange("(p t) one -> p (t one)", t=PACK))
+            return col
+
+        wt_s = zeroed_scales(nc.vector, "wt_s", V)
+        xt_s = zeroed_scales(nc.vector, "xt_s", T)
+        warm_in = pool.tile([P, 1], F32, name="warm_in")
+        warm_out = pool.tile([P, 1], F32, name="warm_out")
+        nc.gpsimd.memset(warm_in[:], 0.0)
+        nc.scalar.activation(warm_out[:], warm_in[:], ACT.Sigmoid)
+
+        sg_t = load_rowwise("sg_t", sg)
+        bg_t = load_rowwise("bg_t", bg)
+        sa_t = load_rowwise("sa_t", sa)
+        wb_s = zeroed_scales(nc.gpsimd, "wb_s", N)
+
+        l2 = load_list("l2", offs2)
+        xt_w = pool.tile([P, T], U16, name="xt_w", align_bytes=64)
+        nc.sync.dma_start(xt_w[:].bitcast(I32), xt_words[0].bitcast(I32))
+        l1 = load_list("l1", offs)
+        load_scales(nc.sync, wt_s, wt_scales)
+        wt_w = pool.tile([P, V], U32, name="wt_w", align_bytes=64)
+        nc.sync.dma_start(wt_w[:].bitcast(I32), wt_words[0].rearrange("p c b -> p (c b)").bitcast(I32))
+        load_scales(nc.sync, xt_s, xt_scales)
+        l5 = load_list("l5", offs5)
+        l4 = load_list("l4", offs4)
+        l3 = load_list("l3", offs3)
+        wb_w = pool.tile([P, N], U32, name="wb_w", align_bytes=64)
+        nc.sync.dma_start(wb_w[:].bitcast(I32), wb_words[0].rearrange("p c b -> p (c b)").bitcast(I32))
+        load_scales(nc.sync, wb_s, wb_scales)
+        so_t = pool.tile([P, N // P], F32, name="so_t")
+        with nc.allow_non_contiguous_dma(reason="one weight for each output feature, one feature a partition"):
+            nc.sync.dma_start(so_t[:], so.rearrange("(h p) one -> p (h one)", p=P))
+        l7 = load_list("l7", offs7)
+        l6 = load_list("l6", offs6)
+
+        boards = []
+        for t in range(PACK):
+            board = pool.tile([P, C], F32, name="board%d" % t)
+            (nc.gpsimd if t == PACK - 1 else nc.vector).memset(board[:], 0.0)
+            boards.append(board)
+
+        xg_w = pool.tile([P, J], U16, name="xg_w", align_bytes=64)
+        xg_s = pool.tile([P, J], U8, name="xg_s", align_bytes=64)
+        wg_w = pool.tile([P, R], U32, name="wg_w", align_bytes=64)
+        wg_s = pool.tile([P, R], U8, name="wg_s", align_bytes=64)
+        nc.vector.tensor_copy(xg_w[:], xt_w[:].indirect(l2[:]))
+        nc.vector.tensor_copy(wg_s[:].rearrange("p (t m) -> p m t", t=PACK), wt_s[:].indirect(l1[:]))
+        nc.vector.tensor_copy(wg_w[:].rearrange("p (t m) -> p m t", t=PACK), wt_w[:].indirect(l1[:]))
+        nc.vector.tensor_copy(xg_s[:], xt_s[:].indirect(l2[:]))
+
+        lin = pool.tile([P, PACK, O], F32, name="lin")
+        gate = pool.tile([P, PACK, O], F32, name="gate")
+
+        def read_board(t, lo, hi):
+            cols = slice(lo // 16, hi // 16)
+            nc.scalar.activation(
+                gate[:, t, lo:hi], boards[t][:].indirect(l5[:, cols]), ACT.Sigmoid,
+                bias=bg_t[:, t : t + 1], scale=sg_t[:, t : t + 1],
+            )
+            nc.scalar.activation(
+                lin[:, t, lo:hi], boards[t][:].indirect(l4[:, cols]), ACT.Copy, scale=sa_t[:, t : t + 1],
+            )
+
+        for t in range(PACK):
+            a_ps = psum.tile([P, J], F32, name="a_ps%d" % t)
+            m_cols = slice(P * t, P * (t + 1))
+            nc.tensor.matmul_mx(
+                out=a_ps[:],
+                lhsT=wg_w[:, m_cols].bitcast(E5M2), lhsT_scale=wg_s[:, m_cols],
+                rhs=xg_w[:].bitcast(E2M1), rhs_scale=xg_s[:],
+                start=True, stop=True,
+            )
+            a_sb = pool.tile([P, J], F32, name="a_sb%d" % t)
+            if t == 0:
+                nc.scalar.copy(a_sb[:], a_ps[:])
+                nc.scalar.activation(boards[t][:].indirect(l3[:]), a_sb[:], ACT.Copy)
+            else:
+                nc.vector.tensor_copy(a_sb[:], a_ps[:])
+                nc.vector.tensor_copy(boards[t][:].indirect(l3[:]), a_sb[:])
+
+        for t in range(PACK - 1):
+            read_board(t, 0, O)
+
+        hid = pool.tile([P, O, PACK], BF16, name="hid", align_bytes=64)
+
+        def gated(t0, lo, hi):
+            nc.vector.tensor_tensor(
+                hid[:, lo:hi, t0 : t0 + 2].rearrange("p (c i) t -> p c t i", i=4),
+                lin[:, t0 : t0 + 2, lo:hi].rearrange("p t (c i) -> p c t i", i=4),
+                gate[:, t0 : t0 + 2, lo:hi].rearrange("p t (c i) -> p c t i", i=4),
+                ALU.mult,
+            )
+
+        gated(0, 0, O)
+        p_sb = [pool.tile([P, O], F32, name="p_sb%d" % h) for h in range(N // P)]
+        for oh in range(2):
+            lo, hi = HALF * oh, HALF * (oh + 1)
+            read_board(PACK - 1, lo, hi)
+            gated(2, lo, hi)
+            hq_w = pool.tile([P, HALF], U32, name="hq_w%d" % oh, align_bytes=64)
+            hq_s = pool.tile([P, HALF], U8, name="hq_s%d" % oh, align_bytes=64)
+            nc.vector.quantize_mx(out=hq_w[:].bitcast(E5M2), scales=hq_s[:], in_=hid[:, lo:hi, :].rearrange("p o t -> p (o t)"))
+            for h in range(N // P):
+                p_ps = psum.tile([P, HALF], F32, name="p_ps%d_%d" % (oh, h))
+                n_cols = slice(P * h, P * (h + 1))
+                nc.tensor.matmul_mx(
+                    out=p_ps[:],
+                    lhsT=wb_w[:, n_cols].bitcast(E4M3), lhsT_scale=wb_s[:, n_cols],
+                    rhs=hq_w[:].bitcast(E5M2), rhs_scale=hq_s[:],
+                    start=True, stop=True,
+                )
+                if oh == 1 and h == 1:
+                    nc.vector.tensor_copy(p_sb[h][:, lo:hi], p_ps[:])
+                else:
+                    nc.scalar.copy(p_sb[h][:, lo:hi], p_ps[:])
+
+        picks = []
+        for h in range(N // P):
+            second = pool.tile([P, U], F32, name="second%d" % h)
+            nc.scalar.activation(second[:], p_sb[h][:].indirect(l7[:]), ACT.Copy, scale=so_t[:, h : h + 1])
+            first = pool.tile([P, U], F32, name="first%d" % h)
+            nc.vector.tensor_copy(first[:], p_sb[h][:].indirect(l6[:]))
+            picks.append((first, second))
+        for h, (first, second) in enumerate(picks):
+            y = pool.tile([P, U], F32, name="y%d" % h)
+            nc.vector.tensor_tensor(y[:], first[:], second[:], ALU.subtract)
+            nc.sync.dma_start(out[P * h : P * (h + 1), :], y[:])

@@ -48,20 +48,16 @@ def tile_list_gatedread_chosen_one_weighedout_kernel(
 
         def load_rowwise(name, src):
             col = pool.tile([P, PACK], F32, name=name)
-            nc.gpsimd.dma_start(col[:], src.rearrange("(p t) one -> p (t one)", t=PACK))
+            nc.sync.dma_start(col[:], src.rearrange("(p t) one -> p (t one)", t=PACK))
             return col
 
         wt_s = zeroed_scales(nc.vector, "wt_s", V)
         xt_s = zeroed_scales(nc.vector, "xt_s", T)
         warm_in = pool.tile([P, 1], F32, name="warm_in")
         warm_out = pool.tile([P, 1], F32, name="warm_out")
-        nc.gpsimd.memset(warm_in[:], 0.0)
+        nc.vector.memset(warm_in[:], 0.0)
         nc.scalar.activation(warm_out[:], warm_in[:], ACT.Sigmoid)
-
-        sg_t = load_rowwise("sg_t", sg)
-        bg_t = load_rowwise("bg_t", bg)
-        sa_t = load_rowwise("sa_t", sa)
-        wb_s = zeroed_scales(nc.gpsimd, "wb_s", N)
+        wb_s = zeroed_scales(nc.vector, "wb_s", N)
 
         l2 = load_list("l2", offs2)
         xt_w = pool.tile([P, T], U16, name="xt_w", align_bytes=64)
@@ -73,6 +69,9 @@ def tile_list_gatedread_chosen_one_weighedout_kernel(
         load_scales(nc.sync, xt_s, xt_scales)
         l5 = load_list("l5", offs5)
         l4 = load_list("l4", offs4)
+        sg_t = load_rowwise("sg_t", sg)
+        bg_t = load_rowwise("bg_t", bg)
+        sa_t = load_rowwise("sa_t", sa)
         l3 = load_list("l3", offs3)
         wb_w = pool.tile([P, N], U32, name="wb_w", align_bytes=64)
         nc.sync.dma_start(wb_w[:].bitcast(I32), wb_words[0].rearrange("p c b -> p (c b)").bitcast(I32))
@@ -86,7 +85,7 @@ def tile_list_gatedread_chosen_one_weighedout_kernel(
         boards = []
         for t in range(PACK):
             board = pool.tile([P, C], F32, name="board%d" % t)
-            (nc.gpsimd if t == PACK - 1 else nc.vector).memset(board[:], 0.0)
+            nc.vector.memset(board[:], 0.0)
             boards.append(board)
 
         xg_w = pool.tile([P, J], U16, name="xg_w", align_bytes=64)
@@ -96,7 +95,9 @@ def tile_list_gatedread_chosen_one_weighedout_kernel(
         nc.vector.tensor_copy(xg_w[:], xt_w[:].indirect(l2[:]))
         nc.vector.tensor_copy(wg_s[:].rearrange("p (t m) -> p m t", t=PACK), wt_s[:].indirect(l1[:]))
         nc.vector.tensor_copy(wg_w[:].rearrange("p (t m) -> p m t", t=PACK), wt_w[:].indirect(l1[:]))
-        nc.vector.tensor_copy(xg_s[:], xt_s[:].indirect(l2[:]))
+        for lo in (0, J // 2):
+            hi = lo + J // 2
+            nc.vector.tensor_copy(xg_s[:, lo:hi], xt_s[:].indirect(l2[:, lo // 16 : hi // 16]))
 
         lin = pool.tile([P, PACK, O], F32, name="lin")
         gate = pool.tile([P, PACK, O], F32, name="gate")
@@ -111,15 +112,25 @@ def tile_list_gatedread_chosen_one_weighedout_kernel(
                 lin[:, t, lo:hi], boards[t][:].indirect(l4[:, cols]), ACT.Copy, scale=sa_t[:, t : t + 1],
             )
 
-        for t in range(PACK):
-            a_ps = psum.tile([P, J], F32, name="a_ps%d" % t)
+        a_banks = [psum.tile([P, J], F32, name="a_ps%d" % t) for t in range(PACK)]
+
+        def first_product(t, lo, hi):
             m_cols = slice(P * t, P * (t + 1))
             nc.tensor.matmul_mx(
-                out=a_ps[:],
+                out=a_banks[t][:, lo:hi],
                 lhsT=wg_w[:, m_cols].bitcast(E5M2), lhsT_scale=wg_s[:, m_cols],
-                rhs=xg_w[:].bitcast(E2M1), rhs_scale=xg_s[:],
+                rhs=xg_w[:, lo:hi].bitcast(E2M1), rhs_scale=xg_s[:, lo:hi],
                 start=True, stop=True,
             )
+
+        for lo in (0, J // 2):
+            for t in (0, 1):
+                first_product(t, lo, lo + J // 2)
+        for t in (2, 3):
+            first_product(t, 0, J)
+
+        for t in range(PACK):
+            a_ps = a_banks[t]
             a_sb = pool.tile([P, J], F32, name="a_sb%d" % t)
             if t == 0:
                 nc.scalar.copy(a_sb[:], a_ps[:])
@@ -133,23 +144,28 @@ def tile_list_gatedread_chosen_one_weighedout_kernel(
 
         hid = pool.tile([P, O, PACK], BF16, name="hid", align_bytes=64)
 
-        def gated(t0, lo, hi):
+        def gated(t0, t1, lo, hi):
             nc.vector.tensor_tensor(
-                hid[:, lo:hi, t0 : t0 + 2].rearrange("p (c i) t -> p c t i", i=4),
-                lin[:, t0 : t0 + 2, lo:hi].rearrange("p t (c i) -> p c t i", i=4),
-                gate[:, t0 : t0 + 2, lo:hi].rearrange("p t (c i) -> p c t i", i=4),
+                hid[:, lo:hi, t0:t1].rearrange("p (c i) t -> p c t i", i=4),
+                lin[:, t0:t1, lo:hi].rearrange("p t (c i) -> p c t i", i=4),
+                gate[:, t0:t1, lo:hi].rearrange("p t (c i) -> p c t i", i=4),
                 ALU.mult,
             )
 
-        gated(0, 0, O)
+        gated(0, 2, HALF, O)
+        read_board(PACK - 1, 0, HALF)
+        gated(0, PACK, 0, HALF)
+        read_board(PACK - 1, HALF, O)
+        gated(2, PACK, HALF, O)
+
         p_sb = [pool.tile([P, O], F32, name="p_sb%d" % h) for h in range(N // P)]
         for oh in range(2):
             lo, hi = HALF * oh, HALF * (oh + 1)
-            read_board(PACK - 1, lo, hi)
-            gated(2, lo, hi)
             hq_w = pool.tile([P, HALF], U32, name="hq_w%d" % oh, align_bytes=64)
             hq_s = pool.tile([P, HALF], U8, name="hq_s%d" % oh, align_bytes=64)
-            nc.vector.quantize_mx(out=hq_w[:].bitcast(E5M2), scales=hq_s[:], in_=hid[:, lo:hi, :].rearrange("p o t -> p (o t)"))
+            nc.vector.quantize_mx(
+                out=hq_w[:].bitcast(E5M2), scales=hq_s[:], in_=hid[:, lo:hi, :].rearrange("p o t -> p (o t)")
+            )
             for h in range(N // P):
                 p_ps = psum.tile([P, HALF], F32, name="p_ps%d_%d" % (oh, h))
                 n_cols = slice(P * h, P * (h + 1))
@@ -159,10 +175,10 @@ def tile_list_gatedread_chosen_one_weighedout_kernel(
                     rhs=hq_w[:].bitcast(E5M2), rhs_scale=hq_s[:],
                     start=True, stop=True,
                 )
-                if oh == 1 and h == 1:
-                    nc.vector.tensor_copy(p_sb[h][:, lo:hi], p_ps[:])
-                else:
+                if h == 0:
                     nc.scalar.copy(p_sb[h][:, lo:hi], p_ps[:])
+                else:
+                    nc.vector.tensor_copy(p_sb[h][:, lo:hi], p_ps[:])
 
         picks = []
         for h in range(N // P):

from contextlib import ExitStack

import concourse.mybir as mybir

K, T, J, R, V, C, O, N, U = 512, 1024, 256, 512, 1024, 512, 256, 256, 128
FLOPS = 2 * K * R * J + 2 * R * N * O

F32 = mybir.dt.float32
BF16 = mybir.dt.bfloat16
I32 = mybir.dt.int32
U32 = mybir.dt.uint32
U16 = mybir.dt.uint16
U8 = mybir.dt.uint8
E2M1 = mybir.dt.float4_e2m1fn_x4
E4M3 = mybir.dt.float8_e4m3fn_x4
E5M2 = mybir.dt.float8_e5m2_x4
ACT = mybir.ActivationFunctionType
ALU = mybir.AluOpType

P = 128
PACK = 4
QUADS = 4
HALF = O // 2


def tile_list_gatedread_chosen_one_weighedout_kernel(
    tc, xt_words, xt_scales, wt_words, wt_scales, sa, sg, bg, wb_words, wb_scales, so,
    offs, offs2, offs3, offs4, offs5, offs6, offs7, out,
):
    nc = tc.nc
    with ExitStack() as ctx:
        pool = ctx.enter_context(tc.tile_pool(name="pool", bufs=1))
        psum = ctx.enter_context(tc.psum_pool(name="psum", bufs=1))

        def load_list(name, src):
            lst = pool.tile(list(src.shape), U16, name=name)
            nc.sync.dma_start(lst[:], src)
            return lst

        def zeroed_scales(engine, name, width):
            rows = pool.tile([P, width], U8, name=name, align_bytes=64)
            engine.memset(rows[:].bitcast(I32), 0)
            return rows

        def load_scales(queue, rows, src):
            for q in range(QUADS):
                queue.dma_start(rows[32 * q : 32 * q + 4, :].bitcast(I32), src[0, 4 * q : 4 * q + 4, :].bitcast(I32))

        def load_rowwise(name, src):
            col = pool.tile([P, PACK], F32, name=name)
            nc.sync.dma_start(col[:], src.rearrange("(p t) one -> p (t one)", t=PACK))
            return col

        wt_s = zeroed_scales(nc.vector, "wt_s", V)
        xt_s = zeroed_scales(nc.vector, "xt_s", T)
        warm_in = pool.tile([P, 1], F32, name="warm_in")
        warm_out = pool.tile([P, 1], F32, name="warm_out")
        nc.vector.memset(warm_in[:], 0.0)
        nc.scalar.activation(warm_out[:], warm_in[:], ACT.Sigmoid)
        wb_s = zeroed_scales(nc.vector, "wb_s", N)

        l2 = load_list("l2", offs2)
        xt_w = pool.tile([P, T], U16, name="xt_w", align_bytes=64)
        nc.sync.dma_start(xt_w[:].bitcast(I32), xt_words[0].bitcast(I32))
        l1 = load_list("l1", offs)
        load_scales(nc.sync, wt_s, wt_scales)
        wt_w = pool.tile([P, V], U32, name="wt_w", align_bytes=64)
        nc.sync.dma_start(wt_w[:].bitcast(I32), wt_words[0].rearrange("p c b -> p (c b)").bitcast(I32))
        load_scales(nc.sync, xt_s, xt_scales)
        l5 = load_list("l5", offs5)
        l4 = load_list("l4", offs4)
        sg_t = load_rowwise("sg_t", sg)
        bg_t = load_rowwise("bg_t", bg)
        sa_t = load_rowwise("sa_t", sa)
        l3 = load_list("l3", offs3)
        wb_w = pool.tile([P, N], U32, name="wb_w", align_bytes=64)
        nc.sync.dma_start(wb_w[:].bitcast(I32), wb_words[0].rearrange("p c b -> p (c b)").bitcast(I32))
        load_scales(nc.sync, wb_s, wb_scales)
        so_t = pool.tile([P, N // P], F32, name="so_t")
        with nc.allow_non_contiguous_dma(reason="one weight for each output feature, one feature a partition"):
            nc.sync.dma_start(so_t[:], so.rearrange("(h p) one -> p (h one)", p=P))
        l7 = load_list("l7", offs7)
        l6 = load_list("l6", offs6)

        boards = []
        for t in range(PACK):
            board = pool.tile([P, C], F32, name="board%d" % t)
            nc.vector.memset(board[:], 0.0)
            boards.append(board)

        xg_w = pool.tile([P, J], U16, name="xg_w", align_bytes=64)
        xg_s = pool.tile([P, J], U8, name="xg_s", align_bytes=64)
        wg_w = pool.tile([P, R], U32, name="wg_w", align_bytes=64)
        wg_s = pool.tile([P, R], U8, name="wg_s", align_bytes=64)
        nc.vector.tensor_copy(xg_w[:], xt_w[:].indirect(l2[:]))
        nc.vector.tensor_copy(wg_s[:].rearrange("p (t m) -> p m t", t=PACK), wt_s[:].indirect(l1[:]))
        nc.vector.tensor_copy(wg_w[:].rearrange("p (t m) -> p m t", t=PACK), wt_w[:].indirect(l1[:]))
        for lo in (0, J // 2):
            hi = lo + J // 2
            nc.vector.tensor_copy(xg_s[:, lo:hi], xt_s[:].indirect(l2[:, lo // 16 : hi // 16]))

        lin = pool.tile([P, PACK, O], F32, name="lin")
        gate = pool.tile([P, PACK, O], F32, name="gate")

        def read_board(t, lo, hi):
            cols = slice(lo // 16, hi // 16)
            nc.scalar.activation(
                gate[:, t, lo:hi], boards[t][:].indirect(l5[:, cols]), ACT.Sigmoid,
                bias=bg_t[:, t : t + 1], scale=sg_t[:, t : t + 1],
            )
            nc.scalar.activation(
                lin[:, t, lo:hi], boards[t][:].indirect(l4[:, cols]), ACT.Copy, scale=sa_t[:, t : t + 1],
            )

        a_banks = [psum.tile([P, J], F32, name="a_ps%d" % t) for t in range(PACK)]

        def first_product(t, lo, hi):
            m_cols = slice(P * t, P * (t + 1))
            nc.tensor.matmul_mx(
                out=a_banks[t][:, lo:hi],
                lhsT=wg_w[:, m_cols].bitcast(E5M2), lhsT_scale=wg_s[:, m_cols],
                rhs=xg_w[:, lo:hi].bitcast(E2M1), rhs_scale=xg_s[:, lo:hi],
                start=True, stop=True,
            )

        for lo in (0, J // 2):
            for t in (0, 1):
                first_product(t, lo, lo + J // 2)
        for t in (2, 3):
            first_product(t, 0, J)

        for t in range(PACK):
            a_ps = a_banks[t]
            a_sb = pool.tile([P, J], F32, name="a_sb%d" % t)
            if t == 0:
                nc.scalar.copy(a_sb[:], a_ps[:])
                nc.scalar.activation(boards[t][:].indirect(l3[:]), a_sb[:], ACT.Copy)
            else:
                nc.vector.tensor_copy(a_sb[:], a_ps[:])
                nc.vector.tensor_copy(boards[t][:].indirect(l3[:]), a_sb[:])

        for t in range(PACK - 1):
            read_board(t, 0, O)

        hid = pool.tile([P, O, PACK], BF16, name="hid", align_bytes=64)

        def gated(t0, t1, lo, hi):
            nc.vector.tensor_tensor(
                hid[:, lo:hi, t0:t1].rearrange("p (c i) t -> p c t i", i=4),
                lin[:, t0:t1, lo:hi].rearrange("p t (c i) -> p c t i", i=4),
                gate[:, t0:t1, lo:hi].rearrange("p t (c i) -> p c t i", i=4),
                ALU.mult,
            )

        gated(0, 2, HALF, O)
        read_board(PACK - 1, 0, HALF)
        gated(0, PACK, 0, HALF)
        read_board(PACK - 1, HALF, O)
        gated(2, PACK, HALF, O)

        p_sb = [pool.tile([P, O], F32, name="p_sb%d" % h) for h in range(N // P)]
        for oh in range(2):
            lo, hi = HALF * oh, HALF * (oh + 1)
            hq_w = pool.tile([P, HALF], U32, name="hq_w%d" % oh, align_bytes=64)
            hq_s = pool.tile([P, HALF], U8, name="hq_s%d" % oh, align_bytes=64)
            nc.vector.quantize_mx(
                out=hq_w[:].bitcast(E5M2), scales=hq_s[:], in_=hid[:, lo:hi, :].rearrange("p o t -> p (o t)")
            )
            for h in range(N // P):
                p_ps = psum.tile([P, HALF], F32, name="p_ps%d_%d" % (oh, h))
                n_cols = slice(P * h, P * (h + 1))
                nc.tensor.matmul_mx(
                    out=p_ps[:],
                    lhsT=wb_w[:, n_cols].bitcast(E4M3), lhsT_scale=wb_s[:, n_cols],
                    rhs=hq_w[:].bitcast(E5M2), rhs_scale=hq_s[:],
                    start=True, stop=True,
                )
                if h == 0:
                    nc.scalar.copy(p_sb[h][:, lo:hi], p_ps[:])
                else:
                    nc.vector.tensor_copy(p_sb[h][:, lo:hi], p_ps[:])

        picks = []
        for h in range(N // P):
            second = pool.tile([P, U], F32, name="second%d" % h)
            nc.scalar.activation(second[:], p_sb[h][:].indirect(l7[:]), ACT.Copy, scale=so_t[:, h : h + 1])
            first = pool.tile([P, U], F32, name="first%d" % h)
            nc.vector.tensor_copy(first[:], p_sb[h][:].indirect(l6[:]))
            picks.append((first, second))
        for h, (first, second) in enumerate(picks):
            y = pool.tile([P, U], F32, name="y%d" % h)
            nc.vector.tensor_tensor(y[:], first[:], second[:], ALU.subtract)
            nc.sync.dma_start(out[P * h : P * (h + 1), :], y[:])
